import numpy as np
import ml_dtypes


def mxq(x, axis, fmt="e4m3"):
    dtype, down = {"e4m3": (ml_dtypes.float8_e4m3fn, 7), "e5m2": (ml_dtypes.float8_e5m2, 14)}[fmt]
    v = np.moveaxis(np.asarray(x, np.float32).astype(ml_dtypes.bfloat16).astype(np.float64), axis, -1)
    blocks = v.reshape(v.shape[:-1] + (-1, 32))
    amax = np.abs(blocks).max(-1, keepdims=True)
    byte = np.maximum(np.where(amax > 0, np.frexp(amax)[1] - 1 + 127, 0) - down, 1)
    scale = np.exp2(byte - 127.0)
    codes = (blocks / scale).astype(np.float32).astype(dtype).astype(np.float64)
    return np.moveaxis((codes * scale).reshape(v.shape), -1, axis)


WIDE = False


def mx_kscale(k):
    if not WIDE:
        return np.ones(k)
    levels = np.array([10, -10, 5, -5, 0])
    if k % 512:
        return np.exp2(np.random.permutation(np.resize(levels, k // 32))).repeat(32)
    a = np.empty((k // 512, 16))
    for p in range(k // 512):
        a[p, :8] = np.random.permutation(np.resize(levels, 8))
        for g in range(8):
            far = levels[np.abs(levels - a[p, g]) >= 10]
            a[p, g + 8] = far[np.random.randint(len(far))]
    return np.exp2(a.ravel()).repeat(32)


def f64(x):
    return np.asarray(x).astype(np.float64)


def striped(idx):
    return np.tile(idx.reshape(-1, 16).T, (8, 1)).astype(np.uint16)


def unstriped(offs):
    return offs[:16].T.reshape(-1).astype(np.int64)


E2M1 = np.array([0.0, 0.5, 1.0, 1.5, 2.0, 3.0, 4.0, 6.0, -0.0, -0.5, -1.0, -1.5, -2.0, -3.0, -4.0, -6.0])


def pack_weight(w, fmt):
    k, n = w.shape
    w = f64(np.asarray(w, np.float32).astype(ml_dtypes.bfloat16)).reshape(k // 32, 32, n)
    amax = np.abs(w).max(1)
    if fmt == "e4m3":
        byte = np.frexp(amax)[1] - 1 + 127 - 7
    else:
        mant, ex = np.frexp(amax / 6.0)
        byte = np.where(mant > 0.5, ex, ex - 1) + 127
    byte = np.clip(np.where(amax > 0, byte, 1), 1, 254)
    scaled = (w * np.exp2(127.0 - byte)[:, None, :]).reshape(k, n).astype(np.float32)
    by_word = np.ascontiguousarray(scaled.reshape(k // 512, 128, 4, n).transpose(0, 1, 3, 2))
    if fmt == "e4m3":
        words = by_word.astype(ml_dtypes.float8_e4m3fn).view(np.uint8)
    else:
        c = by_word.astype(ml_dtypes.float4_e2m1fn).view(np.uint8) & 0xF
        words = (c[..., 0::2] | (c[..., 1::2] << 4)).reshape(k // 512, 128, 2 * n)
    return np.ascontiguousarray(words), np.ascontiguousarray(byte.astype(np.uint8).reshape(k // 512, 16, n))


def unpack_weight(words, scales, fmt):
    g, _, n = scales.shape
    words = np.ascontiguousarray(words).reshape(g, 128, n, -1)
    if fmt == "e4m3":
        vals = words.view(ml_dtypes.float8_e4m3fn).astype(np.float64)
    else:
        nib = np.empty((g, 128, n, 4), np.uint8)
        nib[..., 0::2] = words & 0xF
        nib[..., 1::2] = words >> 4
        vals = E2M1[nib]
    vals = vals * np.repeat(np.exp2(scales.astype(np.float64) - 127.0), 8, axis=1)[..., None]
    return vals.transpose(0, 1, 3, 2).reshape(g * 512, n)


def sigmoid(v):
    return 1.0 / (1.0 + np.exp(-np.maximum(v, -700.0)))


def d_sigmoid(v):
    s = 1.0 / (1.0 + np.exp(-np.maximum(v, -700.0)))
    return s * (1.0 - s)


K, T, E, C, H, N = 128, 512, 16, 128, 512, 512
TOP = 4


def by_expert(wq, xq):
    return np.concatenate([wq[e].T @ xq[:, e * C:(e + 1) * C] for e in range(E)], axis=1)


def setup_inputs():
    n = np.random.standard_normal
    s = mx_kscale(N)[:, None]
    u = mx_kscale(H)
    deal = np.repeat(np.arange(E), C).reshape(TOP, T)[:, np.random.permutation(T)]
    deal = np.take_along_axis(deal, np.argsort(np.random.rand(TOP, T), axis=0), axis=0)
    for _ in range(8):
        s_, t_ = np.random.permutation(T).reshape(2, -1); r = np.random.randint(TOP, size=T // 2); x, y = deal[r, s_].copy(), deal[r, t_].copy()
        ok = ~((deal[:, s_] == y).any(0) | (deal[:, t_] == x).any(0)); deal[r[ok], s_[ok]] = y[ok]; deal[r[ok], t_[ok]] = x[ok]
    order = np.lexsort((np.random.rand(TOP * T), deal.reshape(-1)))
    slot_token = order % T; pos = np.empty(TOP * T, np.int64); pos[order] = np.arange(TOP * T); pos = pos.reshape(TOP, T)
    g = np.random.uniform(0.5, 1.5, (TOP, T)); g = g / g.sum(0)
    w_slot = np.empty(E * C)
    for r in range(TOP): w_slot[pos[r]] = g[r]
    w2 = [pack_weight(m, "e2m1") for m in n((E, N, H)) / np.sqrt(N) / s[None] * u[None, None, :]]
    w1 = [pack_weight(m, "e2m1") for m in n((E, H, K)) / np.sqrt(H) / u[None, :, None]]
    w3 = [pack_weight(m, "e2m1") for m in n((E, H, K)) / np.sqrt(H) / u[None, :, None]]
    return {
        "dyT": (n((N, T)) * s).astype(np.float32),
        "a1": n((H, E * C)).astype(np.float32),
        "a3": n((H, E * C)).astype(np.float32),
        "w2_words": np.stack([m[0] for m in w2]),
        "w2_scales": np.stack([m[1] for m in w2]),
        "w1_words": np.stack([m[0] for m in w1]),
        "w1_scales": np.stack([m[1] for m in w1]),
        "w3_words": np.stack([m[0] for m in w3]),
        "w3_scales": np.stack([m[1] for m in w3]),
        "gate": np.tile(w_slot, (N, 1)).astype(np.float32),
        "offs": striped(slot_token),
        "pos1": striped(pos[0]),
        "pos2": striped(pos[1]),
        "pos3": striped(pos[2]),
        "pos4": striped(pos[3]),
    }


def reference(dyT, a1, a3, w2_words, w2_scales, w1_words, w1_scales, w3_words, w3_scales, gate, offs, pos1, pos2, pos3, pos4):
    idx = unstriped(offs)
    w2 = np.stack([unpack_weight(w2_words[e], w2_scales[e], "e2m1") for e in range(E)])
    w1 = np.stack([unpack_weight(w1_words[e], w1_scales[e], "e2m1") for e in range(E)])
    w3 = np.stack([unpack_weight(w3_words[e], w3_scales[e], "e2m1") for e in range(E)])
    gq = mxq(f64(gate) * f64(dyT)[:, idx], 0, "e4m3")
    dh = by_expert(w2, gq)
    da1 = dh * f64(a3) * d_sigmoid(f64(a1))
    da3 = dh * sigmoid(f64(a1))
    dx = by_expert(w1, mxq(da1, 0, "e4m3")) + by_expert(w3, mxq(da3, 0, "e4m3"))
    return dx[:, unstriped(pos1)] + dx[:, unstriped(pos2)] + dx[:, unstriped(pos3)] + dx[:, unstriped(pos4)]

@@ -1,0 +1,268 @@
+from contextlib import ExitStack
+
+import concourse.mybir as mybir
+from concourse.masks import make_identity
+
+K, T, E, C, H, N = 128, 512, 16, 128, 512, 512
+S = E * C
+FLOPS = 2 * S * (N * H + 2 * H * K)
+BYTES = 4 * (N * T + 2 * H * S + S + K * T) + E * (N * H + 2 * H * K) * 17 // 32 + 2 * 128 * (S + 4 * T) // 16
+
+F32 = mybir.dt.float32
+BF16 = mybir.dt.bfloat16
+I32 = mybir.dt.int32
+U32 = mybir.dt.uint32
+U16 = mybir.dt.uint16
+U8 = mybir.dt.uint8
+FP8X4 = mybir.dt.float8_e4m3fn_x4
+FP4X4 = mybir.dt.float4_e2m1fn_x4
+MULT = mybir.AluOpType.mult
+ADD = mybir.AluOpType.add
+SUB = mybir.AluOpType.subtract
+ACT = mybir.ActivationFunctionType
+
+P = 128
+PACK = 4
+GE = 2
+GS = GE * C
+NG = E // GE
+LE = 4
+LS = LE * C
+NL = E // LE
+
+
+def tile_moe_bdx_glu_sigmoid_kernel(
+    tc, dyT, a1, a3, w2_words, w2_scales, w1_words, w1_scales, w3_words, w3_scales, gate, offs, pos1, pos2, pos3, pos4, out
+):
+    nc = tc.nc
+    with ExitStack() as ctx:
+        keep = ctx.enter_context(tc.tile_pool(name="keep", bufs=1))
+        work = ctx.enter_context(tc.tile_pool(name="work", bufs=2))
+        psum = ctx.enter_context(tc.psum_pool(name="psum", bufs=2))
+
+        offs_sb = keep.tile([P, S // 16], U16, name="offs_sb")
+        pos_sb = [keep.tile([P, T // 16], U16, name=f"pos_sb{r}") for r in range(4)]
+        dy_sb = [keep.tile([P, T], F32, name=f"dy_sb{t}") for t in range(PACK)]
+        gate_sb = [keep.tile([P, LS], F32, name=f"gate_sb{c}") for c in range(NL)]
+        a1_sb = [keep.tile([P, PACK, LS], F32, name=f"a1_sb{c}") for c in range(NL)]
+        a3_sb = [keep.tile([P, PACK, LS], F32, name=f"a3_sb{c}") for c in range(NL)]
+        w2_sb = [keep.tile([P, LE, 2 * H], U8, name=f"w2_sb{c}", align_bytes=64) for c in range(NL)]
+        w1_sb = keep.tile([P, E, 2 * K], U8, name="w1_sb", align_bytes=64)
+        w3_sb = keep.tile([P, E, 2 * K], U8, name="w3_sb", align_bytes=64)
+        w2_sc = keep.tile([P, E, H], U8, name="w2_sc", align_bytes=64)
+        w1_sc = keep.tile([P, E, K], U8, name="w1_sc", align_bytes=64)
+        w3_sc = keep.tile([P, E, K], U8, name="w3_sc", align_bytes=64)
+        ident = keep.tile([P, P], F32, name="ident")
+        minus_half = keep.tile([P, 1], F32, name="minus_half")
+        dx_sb = keep.tile([P, S], F32, name="dx_sb")
+        g_codes = [keep.tile([P, GS], U32, name=f"g_codes{j}", align_bytes=64) for j in range(NG)]
+        g_scales = [keep.tile([P, GS], U8, name=f"g_scales{j}", align_bytes=64) for j in range(NG)]
+
+        for plane in (w2_sc, w1_sc, w3_sc):
+            nc.vector.memset(plane[:].bitcast(I32), 0)
+        nc.vector.memset(minus_half[:], -0.5)
+        make_identity(nc, ident[:])
+
+        dy_v = dyT.rearrange("(p t) w -> p t w", t=PACK)
+        a1_v = a1.rearrange("(p t) w -> p t w", t=PACK)
+        a3_v = a3.rearrange("(p t) w -> p t w", t=PACK)
+
+        def load_words(dst, words, e0, e1):
+            nc.sync.dma_start(out=dst[:].bitcast(I32), in_=words[e0:e1, 0].rearrange("e p b -> p e b").bitcast(I32))
+
+        def load_scales(plane, scales):
+            rows = scales[:, 0].rearrange("e (q r) i -> r q e i", r=4)
+            for r in range(4):
+                nc.sync.dma_start(out=plane[r:P:32, :, :].bitcast(I32), in_=rows[r].bitcast(I32))
+
+        def load_a1(c):
+            nc.sync.dma_start(out=a1_sb[c][:], in_=a1_v[:, :, c * LS : (c + 1) * LS])
+
+        def load_a3(c):
+            nc.sync.dma_start(out=a3_sb[c][:], in_=a3_v[:, :, c * LS : (c + 1) * LS])
+
+        def load_w2(c):
+            load_words(w2_sb[c], w2_words, c * LE, (c + 1) * LE)
+
+        nc.sync.dma_start(offs_sb[:], offs)
+        nc.sync.dma_start(out=dy_sb[0][:], in_=dy_v[:, 0, :])
+        nc.sync.dma_start(out=gate_sb[0][:], in_=gate[0:P, 0:LS])
+        for t in range(1, PACK):
+            nc.sync.dma_start(out=dy_sb[t][:], in_=dy_v[:, t, :])
+        for c in range(1, NL):
+            nc.sync.dma_start(out=gate_sb[c][:], in_=gate[0:P, c * LS : (c + 1) * LS])
+        load_a1(0)
+        load_scales(w2_sc, w2_scales)
+        load_w2(0)
+        load_a3(0)
+        load_a1(1)
+        load_w2(1)
+        load_scales(w1_sc, w1_scales)
+        load_scales(w3_sc, w3_scales)
+        load_words(w1_sb, w1_words, 0, E)
+        load_words(w3_sb, w3_words, 0, E)
+        load_a3(1)
+        for c in range(2, NL):
+            load_a1(c)
+            load_w2(c)
+            load_a3(c)
+        for r, pos in enumerate((pos1, pos2, pos3, pos4)):
+            nc.sync.dma_start(pos_sb[r][:], pos)
+
+        def group_cols(j):
+            c, h = divmod(j, LE // GE)
+            return c, slice(h * GS, (h + 1) * GS)
+
+        staged = {}
+
+        def gather(j):
+            c, cols = group_cols(j)
+            g32 = work.tile([P, PACK, GS], F32, name="g32", tag="g32", bufs=4)
+            for t in range(PACK):
+                window = dy_sb[t][:].indirect(offs_sb[:, j * GS // 16 : (j + 1) * GS // 16])
+                nc.vector.tensor_tensor(g32[:, t, :], window, gate_sb[c][:, cols], MULT)
+            g16 = work.tile([P, GS, PACK], BF16, name="g16", bufs=3, align_bytes=64)
+            nc.scalar.copy(
+                out=g16[:].rearrange("p (c i) t -> p c t i", i=2),
+                in_=g32[:].rearrange("p t (c i) -> p c t i", i=2),
+            )
+            staged["g16", j] = g16
+
+        def quantise_g(j):
+            nc.vector.quantize_mx(
+                out=g_codes[j][:].bitcast(FP8X4),
+                scales=g_scales[j][:],
+                in_=staged["g16", j][:].rearrange("p s t -> p (s t)"),
+            )
+
+        def sigmoid(j):
+            c, cols = group_cols(j)
+            sig = work.tile([P, GS, PACK], F32, name="sig", bufs=4)
+            nc.scalar.activation(
+                out=sig[:].rearrange("p (c i) t -> p c t i", i=2),
+                in_=a1_sb[c][:, :, cols].rearrange("p t (c i) -> p c t i", i=2),
+                func=ACT.Sigmoid,
+            )
+            staged["sig", j] = sig
+
+        def square(j):
+            sig = staged["sig", j]
+            sq = work.tile([P, PACK, GS], F32, name="sq", bufs=4)
+            nc.scalar.activation(
+                out=sq[:].rearrange("p t (c i) -> p c t i", i=2),
+                in_=sig[:].rearrange("p (c i) t -> p c t i", i=2),
+                func=ACT.Square,
+                bias=minus_half[:],
+            )
+            staged["sq", j] = sq
+
+        def slope(j):
+            c, cols = group_cols(j)
+            sq = staged["sq", j]
+            m = work.tile([P, PACK, GS], F32, name="m", tag="g32", bufs=4)
+            nc.vector.scalar_tensor_tensor(m[:], sq[:], 0.25, a3_sb[c][:, :, cols], SUB, MULT)
+            staged["m", j] = m
+
+        def first_product(j):
+            for x in range(GE):
+                e = j * GE + x
+                slots = slice(x * C, (x + 1) * C)
+                dht = psum.tile([P, H], F32, name="dht", bufs=2)
+                nc.tensor.matmul_mx(
+                    out=dht[:],
+                    lhsT=g_codes[j][:, slots].bitcast(FP8X4),
+                    lhsT_scale=g_scales[j][:, slots],
+                    rhs=w2_sb[e // LE][:, e % LE, :].bitcast(FP4X4),
+                    rhs_scale=w2_sc[:, e, :],
+                    start=True,
+                    stop=True,
+                )
+                dht_sb = work.tile([P, PACK, P], F32, name="dht_sb", bufs=6)
+                nc.scalar.copy(out=dht_sb[:], in_=dht[:].rearrange("s (p t) -> s t p", t=PACK))
+                staged["dht", e] = dht_sb
+
+        def turn(j):
+            for x in range(GE):
+                e = j * GE + x
+                dh = psum.tile([P, PACK, C], F32, name="dh", bufs=4)
+                for t in range(PACK):
+                    nc.tensor.transpose(dh[:, t, :], staged["dht", e][:, t, :], ident[:])
+                staged["dh", e] = dh
+
+        def gradients(j):
+            da = work.tile([P, 2, GS, PACK], BF16, name="da", bufs=2, align_bytes=64)
+            for x in range(GE):
+                slots = slice(x * C, (x + 1) * C)
+                dh = staged["dh", j * GE + x]
+                nc.vector.scalar_tensor_tensor(
+                    da[:, 1, slots, :], staged["sig", j][:, slots, :], -1.0, dh[:].rearrange("p t s -> p s t"), MULT, MULT
+                )
+                nc.vector.tensor_tensor(
+                    da[:, 0, slots, :].rearrange("p (c i) t -> p c t i", i=2),
+                    dh[:].rearrange("p t (c i) -> p c t i", i=2),
+                    staged["m", j][:, :, slots].rearrange("p t (c i) -> p c t i", i=2),
+                    MULT,
+                )
+            staged["da", j] = da
+
+        def second_product(j):
+            da_codes = work.tile([P, 2, GS], U32, name="da_codes", bufs=2, align_bytes=64)
+            da_scales = work.tile([P, 2, GS], U8, name="da_scales", bufs=2, align_bytes=64)
+            nc.vector.quantize_mx(
+                out=da_codes[:].rearrange("p m s -> p (m s)").bitcast(FP8X4),
+                scales=da_scales[:].rearrange("p m s -> p (m s)"),
+                in_=staged["da", j][:].rearrange("p m s t -> p (m s t)"),
+            )
+            dx = psum.tile([P, GS], F32, name="dx", bufs=2)
+            for x in range(GE):
+                e = j * GE + x
+                slots = slice(x * C, (x + 1) * C)
+                for which, (words, plane) in enumerate(((w1_sb, w1_sc), (w3_sb, w3_sc))):
+                    nc.tensor.matmul_mx(
+                        out=dx[:, slots],
+                        lhsT=words[:, e, :].bitcast(FP4X4),
+                        lhsT_scale=plane[:, e, :],
+                        rhs=da_codes[:, which, slots].bitcast(FP8X4),
+                        rhs_scale=da_scales[:, which, slots],
+                        start=(which == 0),
+                        stop=(which == 1),
+                    )
+            nc.scalar.activation(out=dx_sb[:, j * GS : (j + 1) * GS], in_=dx[:], func=ACT.Copy, scale=-1.0)
+
+        early = [(sigmoid, 0), (square, 0), (sigmoid, 1), (first_product, 0), (square, 1), (first_product, 1), (turn, 0)]
+        for j in range(NG + 1):
+            if j < NG:
+                gather(j)
+            if j >= 1:
+                quantise_g(j - 1)
+            if 1 <= j < NG:
+                step, group = early[j - 1]
+                step(group)
+
+        slope(0)
+        for j in range(NG + 1):
+            if j + 2 < NG:
+                first_product(j + 2)
+                sigmoid(j + 2)
+                square(j + 2)
+            if j + 1 < NG:
+                turn(j + 1)
+                slope(j + 1)
+            if j < NG:
+                gradients(j)
+            if j >= 1:
+                second_product(j - 1)
+
+        half = T // 2
+        sums = [None, None]
+        for r in range(4):
+            for h in range(2):
+                window = dx_sb[:].indirect(pos_sb[r][:, h * half // 16 : (h + 1) * half // 16])
+                acc = work.tile([P, half], F32, name="acc", bufs=4)
+                if r == 0:
+                    nc.vector.tensor_copy(acc[:], window)
+                else:
+                    nc.vector.tensor_tensor(acc[:], window, sums[h][:], ADD)
+                sums[h] = acc
+                if r == 3:
+                    nc.sync.dma_start(out=out[:, h * half : (h + 1) * half], in_=acc[:])

@@ -49,7 +49,8 @@ def tile_moe_bdx_glu_sigmoid_kernel(
         w2_sb = [keep.tile([P, LE, 2 * H], U8, name=f"w2_sb{c}", align_bytes=64) for c in range(NL)]
         w1_sb = keep.tile([P, E, 2 * K], U8, name="w1_sb", align_bytes=64)
         w3_sb = keep.tile([P, E, 2 * K], U8, name="w3_sb", align_bytes=64)
-        w2_sc = keep.tile([P, E, H], U8, name="w2_sc", align_bytes=64)
+        w2_sc_first = keep.tile([P, LE, H], U8, name="w2_sc_first", align_bytes=64)
+        w2_sc_rest = keep.tile([P, E - LE, H], U8, name="w2_sc_rest", align_bytes=64)
         w1_sc = keep.tile([P, E, K], U8, name="w1_sc", align_bytes=64)
         w3_sc = keep.tile([P, E, K], U8, name="w3_sc", align_bytes=64)
         ident = keep.tile([P, P], F32, name="ident")
@@ -58,7 +59,7 @@ def tile_moe_bdx_glu_sigmoid_kernel(
         g_codes = [keep.tile([P, GS], U32, name=f"g_codes{j}", align_bytes=64) for j in range(NG)]
         g_scales = [keep.tile([P, GS], U8, name=f"g_scales{j}", align_bytes=64) for j in range(NG)]
 
-        for plane in (w2_sc, w1_sc, w3_sc):
+        for plane in (w2_sc_first, w2_sc_rest, w1_sc, w3_sc):
             nc.vector.memset(plane[:].bitcast(I32), 0)
         nc.vector.memset(minus_half[:], -0.5)
         make_identity(nc, ident[:])
@@ -75,6 +76,9 @@ def tile_moe_bdx_glu_sigmoid_kernel(
             for r in range(4):
                 nc.sync.dma_start(out=plane[r:P:32, :, :].bitcast(I32), in_=rows[r].bitcast(I32))
 
+        def load_gate(c):
+            nc.sync.dma_start(out=gate_sb[c][:], in_=gate[0:P, c * LS : (c + 1) * LS])
+
         def load_a1(c):
             nc.sync.dma_start(out=a1_sb[c][:], in_=a1_v[:, :, c * LS : (c + 1) * LS])
 
@@ -86,26 +90,30 @@ def tile_moe_bdx_glu_sigmoid_kernel(
 
         nc.sync.dma_start(offs_sb[:], offs)
         nc.sync.dma_start(out=dy_sb[0][:], in_=dy_v[:, 0, :])
-        nc.sync.dma_start(out=gate_sb[0][:], in_=gate[0:P, 0:LS])
+        load_gate(0)
         for t in range(1, PACK):
             nc.sync.dma_start(out=dy_sb[t][:], in_=dy_v[:, t, :])
-        for c in range(1, NL):
-            nc.sync.dma_start(out=gate_sb[c][:], in_=gate[0:P, c * LS : (c + 1) * LS])
         load_a1(0)
-        load_scales(w2_sc, w2_scales)
+        load_gate(1)
+        load_scales(w2_sc_first, w2_scales[0:LE])
         load_w2(0)
-        load_a3(0)
+        load_gate(2)
+        load_gate(3)
         load_a1(1)
+        load_a3(0)
+        load_scales(w2_sc_rest, w2_scales[LE:E])
         load_w2(1)
+        load_a1(2)
+        load_a3(1)
+        load_w2(2)
+        load_a1(3)
         load_scales(w1_sc, w1_scales)
         load_scales(w3_sc, w3_scales)
         load_words(w1_sb, w1_words, 0, E)
         load_words(w3_sb, w3_words, 0, E)
-        load_a3(1)
-        for c in range(2, NL):
-            load_a1(c)
-            load_w2(c)
-            load_a3(c)
+        load_w2(3)
+        load_a3(2)
+        load_a3(3)
         for r, pos in enumerate((pos1, pos2, pos3, pos4)):
             nc.sync.dma_start(pos_sb[r][:], pos)
 
@@ -121,7 +129,10 @@ def tile_moe_bdx_glu_sigmoid_kernel(
             for t in range(PACK):
                 window = dy_sb[t][:].indirect(offs_sb[:, j * GS // 16 : (j + 1) * GS // 16])
                 nc.vector.tensor_tensor(g32[:, t, :], window, gate_sb[c][:, cols], MULT)
-            g16 = work.tile([P, GS, PACK], BF16, name="g16", bufs=3, align_bytes=64)
+            if j >= NG - 2:
+                g16 = work.tile([P, GS, PACK], BF16, name="g16", tag=f"ring{j - NG + 3}", bufs=1, align_bytes=64)
+            else:
+                g16 = work.tile([P, GS, PACK], BF16, name="g16", bufs=3, align_bytes=64)
             nc.scalar.copy(
                 out=g16[:].rearrange("p (c i) t -> p c t i", i=2),
                 in_=g32[:].rearrange("p t (c i) -> p c t i", i=2),
@@ -147,7 +158,7 @@ def tile_moe_bdx_glu_sigmoid_kernel(
 
         def square(j):
             sig = staged["sig", j]
-            sq = work.tile([P, PACK, GS], F32, name="sq", bufs=4)
+            sq = work.tile([P, PACK, GS], F32, name="sq", tag=f"pair{j % 4}", bufs=1, align_bytes=64)
             nc.scalar.activation(
                 out=sq[:].rearrange("p t (c i) -> p c t i", i=2),
                 in_=sig[:].rearrange("p (c i) t -> p c t i", i=2),
@@ -156,11 +167,18 @@ def tile_moe_bdx_glu_sigmoid_kernel(
             )
             staged["sq", j] = sq
 
+        def shift(j):
+            ds = work.tile([P, PACK, GS], F32, name="ds", tag=f"ring{2 * j % 3}", bufs=1, align_bytes=64)
+            nc.vector.tensor_scalar_add(ds[:], staged["sq", j][:], -0.25)
+            staged["ds", j] = ds
+
         def slope(j):
             c, cols = group_cols(j)
-            sq = staged["sq", j]
-            m = work.tile([P, PACK, GS], F32, name="m", tag="g32", bufs=4)
-            nc.vector.scalar_tensor_tensor(m[:], sq[:], 0.25, a3_sb[c][:, :, cols], SUB, MULT)
+            m = work.tile([P, PACK, GS], F32, name="m", tag=f"ring{(2 * j + 1) % 3}", bufs=1, align_bytes=64)
+            if j == 0:
+                nc.vector.scalar_tensor_tensor(m[:], staged["sq", j][:], 0.25, a3_sb[c][:, :, cols], SUB, MULT)
+            else:
+                nc.gpsimd.tensor_tensor(m[:], staged["ds", j][:], a3_sb[c][:, :, cols], MULT)
             staged["m", j] = m
 
         def first_product(j):
@@ -173,11 +191,14 @@ def tile_moe_bdx_glu_sigmoid_kernel(
                     lhsT=g_codes[j][:, slots].bitcast(FP8X4),
                     lhsT_scale=g_scales[j][:, slots],
                     rhs=w2_sb[e // LE][:, e % LE, :].bitcast(FP4X4),
-                    rhs_scale=w2_sc[:, e, :],
+                    rhs_scale=w2_sc_first[:, e, :] if e < LE else w2_sc_rest[:, e - LE, :],
                     start=True,
                     stop=True,
                 )
-                dht_sb = work.tile([P, PACK, P], F32, name="dht_sb", bufs=6)
+                if e in (1, 3):
+                    dht_sb = work.tile([P, PACK, P], F32, name="dht_sb", tag=f"ring{(e + 1) // 2}", bufs=1, align_bytes=64)
+                else:
+                    dht_sb = work.tile([P, PACK, P], F32, name="dht_sb", bufs=4)
                 nc.scalar.copy(out=dht_sb[:], in_=dht[:].rearrange("s (p t) -> s t p", t=PACK))
                 staged["dht", e] = dht_sb
 
@@ -190,15 +211,18 @@ def tile_moe_bdx_glu_sigmoid_kernel(
                 staged["dh", e] = dh
 
         def gradients(j):
-            da = work.tile([P, 2, GS, PACK], BF16, name="da", bufs=2, align_bytes=64)
+            da = work.tile([P, GE, 2, C, PACK], BF16, name="da", tag=f"pair{(j + 1) % 4}", bufs=1, align_bytes=64)
             for x in range(GE):
                 slots = slice(x * C, (x + 1) * C)
                 dh = staged["dh", j * GE + x]
                 nc.vector.scalar_tensor_tensor(
-                    da[:, 1, slots, :], staged["sig", j][:, slots, :], -1.0, dh[:].rearrange("p t s -> p s t"), MULT, MULT
+                    da[:, x, 1], staged["sig", j][:, slots, :], -1.0, dh[:].rearrange("p t s -> p s t"), MULT, MULT
                 )
+            for x in range(GE):
+                slots = slice(x * C, (x + 1) * C)
+                dh = staged["dh", j * GE + x]
                 nc.vector.tensor_tensor(
-                    da[:, 0, slots, :].rearrange("p (c i) t -> p c t i", i=2),
+                    da[:, x, 0].rearrange("p (c i) t -> p c t i", i=2),
                     dh[:].rearrange("p t (c i) -> p c t i", i=2),
                     staged["m", j][:, :, slots].rearrange("p t (c i) -> p c t i", i=2),
                     MULT,
@@ -206,12 +230,12 @@ def tile_moe_bdx_glu_sigmoid_kernel(
             staged["da", j] = da
 
         def second_product(j):
-            da_codes = work.tile([P, 2, GS], U32, name="da_codes", bufs=2, align_bytes=64)
-            da_scales = work.tile([P, 2, GS], U8, name="da_scales", bufs=2, align_bytes=64)
+            da_codes = work.tile([P, GE, 2, C], U32, name="da_codes", bufs=2, align_bytes=64)
+            da_scales = work.tile([P, GE, 2, C], U8, name="da_scales", bufs=2, align_bytes=64)
             nc.vector.quantize_mx(
-                out=da_codes[:].rearrange("p m s -> p (m s)").bitcast(FP8X4),
-                scales=da_scales[:].rearrange("p m s -> p (m s)"),
-                in_=staged["da", j][:].rearrange("p m s t -> p (m s t)"),
+                out=da_codes[:].rearrange("p x m s -> p (x m s)").bitcast(FP8X4),
+                scales=da_scales[:].rearrange("p x m s -> p (x m s)"),
+                in_=staged["da", j][:].rearrange("p x m s t -> p (x m s t)"),
             )
             dx = psum.tile([P, GS], F32, name="dx", bufs=2)
             for x in range(GE):
@@ -222,31 +246,42 @@ def tile_moe_bdx_glu_sigmoid_kernel(
                         out=dx[:, slots],
                         lhsT=words[:, e, :].bitcast(FP4X4),
                         lhsT_scale=plane[:, e, :],
-                        rhs=da_codes[:, which, slots].bitcast(FP8X4),
-                        rhs_scale=da_scales[:, which, slots],
+                        rhs=da_codes[:, x, which, :].bitcast(FP8X4),
+                        rhs_scale=da_scales[:, x, which, :],
                         start=(which == 0),
                         stop=(which == 1),
                     )
             nc.scalar.activation(out=dx_sb[:, j * GS : (j + 1) * GS], in_=dx[:], func=ACT.Copy, scale=-1.0)
 
-        early = [(sigmoid, 0), (square, 0), (sigmoid, 1), (first_product, 0), (square, 1), (first_product, 1), (turn, 0)]
+        early = [
+            [(sigmoid, 0)],
+            [(square, 0)],
+            [(first_product, 0), (turn, 0)],
+            [(sigmoid, 1), (square, 1)],
+            [(first_product, 1), (turn, 1)],
+            [(sigmoid, 2)],
+            [(square, 2)],
+        ]
         for j in range(NG + 1):
             if j < NG:
                 gather(j)
             if j >= 1:
                 quantise_g(j - 1)
             if 1 <= j < NG:
-                step, group = early[j - 1]
-                step(group)
+                for step, group in early[j - 1]:
+                    step(group)
 
         slope(0)
         for j in range(NG + 1):
             if j + 2 < NG:
                 first_product(j + 2)
-                sigmoid(j + 2)
-                square(j + 2)
-            if j + 1 < NG:
+            if j + 3 < NG:
+                sigmoid(j + 3)
+                square(j + 3)
+            if 1 < j + 1 < NG:
                 turn(j + 1)
+            if j + 1 < NG:
+                shift(j + 1)
                 slope(j + 1)
             if j < NG:
                 gradients(j)

@@ -43,12 +43,14 @@ def tile_moe_bdx_glu_sigmoid_kernel(
         offs_sb = keep.tile([P, S // 16], U16, name="offs_sb")
         pos_sb = [keep.tile([P, T // 16], U16, name=f"pos_sb{r}") for r in range(4)]
         dy_sb = [keep.tile([P, T], F32, name=f"dy_sb{t}") for t in range(PACK)]
-        gate_sb = [keep.tile([P, LS], F32, name=f"gate_sb{c}") for c in range(NL)]
-        a1_sb = [keep.tile([P, PACK, LS], F32, name=f"a1_sb{c}") for c in range(NL)]
+        gate_cuts = [0, LS, 2 * LS, 3 * LS, S]
+        gate_sb = [keep.tile([P, gate_cuts[c + 1] - gate_cuts[c]], F32, name=f"gate_sb{c}") for c in range(4)]
+        a1_cuts = [0, GS, LS, 2 * LS, 3 * LS, S]
+        a1_sb = [keep.tile([P, PACK, a1_cuts[c + 1] - a1_cuts[c]], F32, name=f"a1_sb{c}") for c in range(5)]
         a3_sb = [keep.tile([P, PACK, LS], F32, name=f"a3_sb{c}") for c in range(NL)]
         w2_sb = [keep.tile([P, LE, 2 * H], U8, name=f"w2_sb{c}", align_bytes=64) for c in range(NL)]
-        w1_sb = keep.tile([P, E, 2 * K], U8, name="w1_sb", align_bytes=64)
-        w3_sb = keep.tile([P, E, 2 * K], U8, name="w3_sb", align_bytes=64)
+        w1_sb = [keep.tile([P, E // 2, 2 * K], U8, name=f"w1_sb{c}", align_bytes=64) for c in range(2)]
+        w3_sb = [keep.tile([P, E // 2, 2 * K], U8, name=f"w3_sb{c}", align_bytes=64) for c in range(2)]
         w2_sc_first = keep.tile([P, LE, H], U8, name="w2_sc_first", align_bytes=64)
         w2_sc_rest = keep.tile([P, E - LE, H], U8, name="w2_sc_rest", align_bytes=64)
         w1_sc = keep.tile([P, E, K], U8, name="w1_sc", align_bytes=64)
@@ -77,10 +79,10 @@ def tile_moe_bdx_glu_sigmoid_kernel(
                 nc.sync.dma_start(out=plane[r:P:32, :, :].bitcast(I32), in_=rows[r].bitcast(I32))
 
         def load_gate(c):
-            nc.sync.dma_start(out=gate_sb[c][:], in_=gate[0:P, c * LS : (c + 1) * LS])
+            nc.sync.dma_start(out=gate_sb[c][:], in_=gate[0:P, gate_cuts[c] : gate_cuts[c + 1]])
 
         def load_a1(c):
-            nc.sync.dma_start(out=a1_sb[c][:], in_=a1_v[:, :, c * LS : (c + 1) * LS])
+            nc.sync.dma_start(out=a1_sb[c][:], in_=a1_v[:, :, a1_cuts[c] : a1_cuts[c + 1]])
 
         def load_a3(c):
             nc.sync.dma_start(out=a3_sb[c][:], in_=a3_v[:, :, c * LS : (c + 1) * LS])
@@ -91,28 +93,32 @@ def tile_moe_bdx_glu_sigmoid_kernel(
         nc.sync.dma_start(offs_sb[:], offs)
         nc.sync.dma_start(out=dy_sb[0][:], in_=dy_v[:, 0, :])
         load_gate(0)
-        for t in range(1, PACK):
-            nc.sync.dma_start(out=dy_sb[t][:], in_=dy_v[:, t, :])
+        nc.sync.dma_start(out=dy_sb[1][:], in_=dy_v[:, 1, :])
         load_a1(0)
+        for t in range(2, PACK):
+            nc.sync.dma_start(out=dy_sb[t][:], in_=dy_v[:, t, :])
+        load_a1(1)
         load_gate(1)
         load_scales(w2_sc_first, w2_scales[0:LE])
         load_w2(0)
         load_gate(2)
         load_gate(3)
-        load_a1(1)
+        load_a1(2)
         load_a3(0)
         load_scales(w2_sc_rest, w2_scales[LE:E])
         load_w2(1)
-        load_a1(2)
+        load_a1(3)
         load_a3(1)
         load_w2(2)
-        load_a1(3)
+        load_a1(4)
         load_scales(w1_sc, w1_scales)
         load_scales(w3_sc, w3_scales)
-        load_words(w1_sb, w1_words, 0, E)
-        load_words(w3_sb, w3_words, 0, E)
+        load_words(w1_sb[0], w1_words, 0, E // 2)
+        load_words(w3_sb[0], w3_words, 0, E // 2)
         load_w2(3)
         load_a3(2)
+        load_words(w1_sb[1], w1_words, E // 2, E)
+        load_words(w3_sb[1], w3_words, E // 2, E)
         load_a3(3)
         for r, pos in enumerate((pos1, pos2, pos3, pos4)):
             nc.sync.dma_start(pos_sb[r][:], pos)
@@ -123,14 +129,19 @@ def tile_moe_bdx_glu_sigmoid_kernel(
 
         staged = {}
 
-        def gather(j):
+        def gather_plane(j, t):
             c, cols = group_cols(j)
-            g32 = work.tile([P, PACK, GS], F32, name="g32", tag="g32", bufs=4)
-            for t in range(PACK):
-                window = dy_sb[t][:].indirect(offs_sb[:, j * GS // 16 : (j + 1) * GS // 16])
-                nc.vector.tensor_tensor(g32[:, t, :], window, gate_sb[c][:, cols], MULT)
+            if t == 0:
+                staged["g32", j] = work.tile([P, PACK, GS], F32, name="g32", tag="g32", bufs=4)
+            window = dy_sb[t][:].indirect(offs_sb[:, j * GS // 16 : (j + 1) * GS // 16])
+            nc.vector.tensor_tensor(staged["g32", j][:, t, :], window, gate_sb[c][:, cols], MULT)
+
+        def gather(j):
+            for t in range(PACK - 1 if j < 2 else 0, PACK):
+                gather_plane(j, t)
+            g32 = staged["g32", j]
             if j >= NG - 2:
-                g16 = work.tile([P, GS, PACK], BF16, name="g16", tag=f"ring{j - NG + 3}", bufs=1, align_bytes=64)
+                g16 = work.tile([P, GS, PACK], BF16, name="g16", tag=("m0", "sig5")[j - NG + 2], bufs=1, align_bytes=64)
             else:
                 g16 = work.tile([P, GS, PACK], BF16, name="g16", bufs=3, align_bytes=64)
             nc.scalar.copy(
@@ -147,8 +158,9 @@ def tile_moe_bdx_glu_sigmoid_kernel(
             )
 
         def sigmoid(j):
-            c, cols = group_cols(j)
-            sig = work.tile([P, GS, PACK], F32, name="sig", bufs=4)
+            c = max(n for n in range(5) if a1_cuts[n] <= j * GS)
+            cols = slice(j * GS - a1_cuts[c], (j + 1) * GS - a1_cuts[c])
+            sig = work.tile([P, GS, PACK], F32, name="sig", tag=f"sig{j % 6}", bufs=1, align_bytes=64)
             nc.scalar.activation(
                 out=sig[:].rearrange("p (c i) t -> p c t i", i=2),
                 in_=a1_sb[c][:, :, cols].rearrange("p t (c i) -> p c t i", i=2),
@@ -158,7 +170,7 @@ def tile_moe_bdx_glu_sigmoid_kernel(
 
         def square(j):
             sig = staged["sig", j]
-            sq = work.tile([P, PACK, GS], F32, name="sq", tag=f"pair{j % 4}", bufs=1, align_bytes=64)
+            sq = work.tile([P, PACK, GS], F32, name="sq", tag=f"pair{j % 5}", bufs=1, align_bytes=64)
             nc.scalar.activation(
                 out=sq[:].rearrange("p t (c i) -> p c t i", i=2),
                 in_=sig[:].rearrange("p (c i) t -> p c t i", i=2),
@@ -168,13 +180,13 @@ def tile_moe_bdx_glu_sigmoid_kernel(
             staged["sq", j] = sq
 
         def shift(j):
-            ds = work.tile([P, PACK, GS], F32, name="ds", tag=f"ring{2 * j % 3}", bufs=1, align_bytes=64)
+            ds = work.tile([P, PACK, GS], F32, name="ds", tag=f"sig{(j - 2) % 6}", bufs=1, align_bytes=64)
             nc.vector.tensor_scalar_add(ds[:], staged["sq", j][:], -0.25)
             staged["ds", j] = ds
 
         def slope(j):
             c, cols = group_cols(j)
-            m = work.tile([P, PACK, GS], F32, name="m", tag=f"ring{(2 * j + 1) % 3}", bufs=1, align_bytes=64)
+            m = work.tile([P, PACK, GS], F32, name="m", tag=f"m{j % 2}", bufs=1, align_bytes=64)
             if j == 0:
                 nc.vector.scalar_tensor_tensor(m[:], staged["sq", j][:], 0.25, a3_sb[c][:, :, cols], SUB, MULT)
             else:
@@ -196,7 +208,7 @@ def tile_moe_bdx_glu_sigmoid_kernel(
                     stop=True,
                 )
                 if e in (1, 3):
-                    dht_sb = work.tile([P, PACK, P], F32, name="dht_sb", tag=f"ring{(e + 1) // 2}", bufs=1, align_bytes=64)
+                    dht_sb = work.tile([P, PACK, P], F32, name="dht_sb", tag=("m0", "sig5")[e // 2], bufs=1, align_bytes=64)
                 else:
                     dht_sb = work.tile([P, PACK, P], F32, name="dht_sb", bufs=4)
                 nc.scalar.copy(out=dht_sb[:], in_=dht[:].rearrange("s (p t) -> s t p", t=PACK))
@@ -211,7 +223,7 @@ def tile_moe_bdx_glu_sigmoid_kernel(
                 staged["dh", e] = dh
 
         def gradients(j):
-            da = work.tile([P, GE, 2, C, PACK], BF16, name="da", tag=f"pair{(j + 1) % 4}", bufs=1, align_bytes=64)
+            da = work.tile([P, GE, 2, C, PACK], BF16, name="da", tag=f"pair{(j + 1) % 5}", bufs=1, align_bytes=64)
             for x in range(GE):
                 slots = slice(x * C, (x + 1) * C)
                 dh = staged["dh", j * GE + x]
@@ -229,39 +241,50 @@ def tile_moe_bdx_glu_sigmoid_kernel(
                 )
             staged["da", j] = da
 
-        def second_product(j):
-            da_codes = work.tile([P, GE, 2, C], U32, name="da_codes", bufs=2, align_bytes=64)
-            da_scales = work.tile([P, GE, 2, C], U8, name="da_scales", bufs=2, align_bytes=64)
+        def quantise_da(j, x0, x1):
+            width = x1 - x0
+            da_codes = work.tile([P, width, 2, C], U32, name="da_codes", bufs=3, align_bytes=64)
+            da_scales = work.tile([P, width, 2, C], U8, name="da_scales", bufs=3, align_bytes=64)
             nc.vector.quantize_mx(
                 out=da_codes[:].rearrange("p x m s -> p (x m s)").bitcast(FP8X4),
                 scales=da_scales[:].rearrange("p x m s -> p (x m s)"),
-                in_=staged["da", j][:].rearrange("p x m s t -> p (x m s t)"),
+                in_=staged["da", j][:, x0:x1].rearrange("p x m s t -> p (x m s t)"),
             )
-            dx = psum.tile([P, GS], F32, name="dx", bufs=2)
-            for x in range(GE):
-                e = j * GE + x
-                slots = slice(x * C, (x + 1) * C)
+            staged["codes", j, x0] = (da_codes, da_scales)
+
+        def second_product(j, x0, x1):
+            width = x1 - x0
+            da_codes, da_scales = staged["codes", j, x0]
+            dx = psum.tile([P, width * C], F32, name="dx", bufs=2)
+            for x in range(width):
+                e = j * GE + x0 + x
                 for which, (words, plane) in enumerate(((w1_sb, w1_sc), (w3_sb, w3_sc))):
                     nc.tensor.matmul_mx(
-                        out=dx[:, slots],
-                        lhsT=words[:, e, :].bitcast(FP4X4),
+                        out=dx[:, x * C : (x + 1) * C],
+                        lhsT=words[e // (E // 2)][:, e % (E // 2), :].bitcast(FP4X4),
                         lhsT_scale=plane[:, e, :],
                         rhs=da_codes[:, x, which, :].bitcast(FP8X4),
                         rhs_scale=da_scales[:, x, which, :],
                         start=(which == 0),
                         stop=(which == 1),
                     )
-            nc.scalar.activation(out=dx_sb[:, j * GS : (j + 1) * GS], in_=dx[:], func=ACT.Copy, scale=-1.0)
+            first = (j * GE + x0) * C
+            nc.scalar.activation(out=dx_sb[:, first : first + width * C], in_=dx[:], func=ACT.Copy, scale=-1.0)
 
         early = [
-            [(sigmoid, 0)],
-            [(square, 0)],
+            [(sigmoid, 1)],
+            [(square, 1)],
             [(first_product, 0), (turn, 0)],
-            [(sigmoid, 1), (square, 1)],
+            [(sigmoid, 2), (square, 2)],
             [(first_product, 1), (turn, 1)],
-            [(sigmoid, 2)],
-            [(square, 2)],
+            [(sigmoid, 3)],
+            [(square, 3)],
         ]
+        for t in range(PACK - 1):
+            gather_plane(0, t)
+            gather_plane(1, t)
+        sigmoid(0)
+        square(0)
         for j in range(NG + 1):
             if j < NG:
                 gather(j)
@@ -272,28 +295,36 @@ def tile_moe_bdx_glu_sigmoid_kernel(
                     step(group)
 
         slope(0)
-        for j in range(NG + 1):
-            if j + 2 < NG:
-                first_product(j + 2)
-            if j + 3 < NG:
-                sigmoid(j + 3)
-                square(j + 3)
-            if 1 < j + 1 < NG:
-                turn(j + 1)
+        for j in range(NG):
             if j + 1 < NG:
                 shift(j + 1)
                 slope(j + 1)
-            if j < NG:
-                gradients(j)
-            if j >= 1:
-                second_product(j - 1)
+            if j >= 2:
+                quantise_da(j - 2, 0, GE)
+            if j == NG - 1:
+                quantise_da(j - 1, 0, GE)
+            if j + 2 < NG:
+                first_product(j + 2)
+            if j + 4 < NG:
+                sigmoid(j + 4)
+                square(j + 4)
+            if 1 < j + 1 < NG:
+                turn(j + 1)
+            if j >= 2:
+                second_product(j - 2, 0, GE)
+            if j == NG - 1:
+                second_product(j - 1, 0, GE)
+            gradients(j)
+        for x in range(GE):
+            quantise_da(NG - 1, x, x + 1)
+            second_product(NG - 1, x, x + 1)
 
         half = T // 2
         sums = [None, None]
         for r in range(4):
             for h in range(2):
                 window = dx_sb[:].indirect(pos_sb[r][:, h * half // 16 : (h + 1) * half // 16])
-                acc = work.tile([P, half], F32, name="acc", bufs=4)
+                acc = work.tile([P, half], F32, name="acc", tag="g32", bufs=4)
                 if r == 0:
                     nc.vector.tensor_copy(acc[:], window)
                 else:

@@ -117,9 +117,9 @@ def tile_moe_bdx_glu_sigmoid_kernel(
         load_words(w3_sb[0], w3_words, 0, E // 2)
         load_w2(3)
         load_a3(2)
+        load_a3(3)
         load_words(w1_sb[1], w1_words, E // 2, E)
         load_words(w3_sb[1], w3_words, E // 2, E)
-        load_a3(3)
         for r, pos in enumerate((pos1, pos2, pos3, pos4)):
             nc.sync.dma_start(pos_sb[r][:], pos)
 
@@ -141,7 +141,7 @@ def tile_moe_bdx_glu_sigmoid_kernel(
                 gather_plane(j, t)
             g32 = staged["g32", j]
             if j >= NG - 2:
-                g16 = work.tile([P, GS, PACK], BF16, name="g16", tag=("m0", "sig5")[j - NG + 2], bufs=1, align_bytes=64)
+                g16 = work.tile([P, GS, PACK], BF16, name="g16", tag=("m0", "sig6")[j - NG + 2], bufs=1, align_bytes=64)
             else:
                 g16 = work.tile([P, GS, PACK], BF16, name="g16", bufs=3, align_bytes=64)
             nc.scalar.copy(
@@ -160,7 +160,7 @@ def tile_moe_bdx_glu_sigmoid_kernel(
         def sigmoid(j):
             c = max(n for n in range(5) if a1_cuts[n] <= j * GS)
             cols = slice(j * GS - a1_cuts[c], (j + 1) * GS - a1_cuts[c])
-            sig = work.tile([P, GS, PACK], F32, name="sig", tag=f"sig{j % 6}", bufs=1, align_bytes=64)
+            sig = work.tile([P, GS, PACK], F32, name="sig", tag=f"sig{j % 7}", bufs=1, align_bytes=64)
             nc.scalar.activation(
                 out=sig[:].rearrange("p (c i) t -> p c t i", i=2),
                 in_=a1_sb[c][:, :, cols].rearrange("p t (c i) -> p c t i", i=2),
@@ -179,18 +179,18 @@ def tile_moe_bdx_glu_sigmoid_kernel(
             )
             staged["sq", j] = sq
 
-        def shift(j):
-            ds = work.tile([P, PACK, GS], F32, name="ds", tag=f"sig{(j - 2) % 6}", bufs=1, align_bytes=64)
-            nc.vector.tensor_scalar_add(ds[:], staged["sq", j][:], -0.25)
-            staged["ds", j] = ds
-
         def slope(j):
             c, cols = group_cols(j)
-            m = work.tile([P, PACK, GS], F32, name="m", tag=f"m{j % 2}", bufs=1, align_bytes=64)
+            sq = staged["sq", j]
+            a3_cols = a3_sb[c][:, :, cols]
             if j == 0:
-                nc.vector.scalar_tensor_tensor(m[:], staged["sq", j][:], 0.25, a3_sb[c][:, :, cols], SUB, MULT)
+                m = work.tile([P, PACK, GS], F32, name="m", tag="m0", bufs=1, align_bytes=64)
+                nc.vector.scalar_tensor_tensor(m[:], sq[:], 0.25, a3_cols, SUB, MULT)
             else:
-                nc.gpsimd.tensor_tensor(m[:], staged["ds", j][:], a3_sb[c][:, :, cols], MULT)
+                m = work.tile([P, PACK, GS], F32, name="m", tag=f"sig{(j - 2) % 7}", bufs=1, align_bytes=64)
+                nc.vector.scalar_tensor_tensor(m[:, 3:, :], sq[:, 3:, :], 0.25, a3_cols[:, 3:, :], SUB, MULT)
+                nc.vector.tensor_scalar_add(m[:, :3, :], sq[:, :3, :], -0.25)
+                nc.gpsimd.tensor_tensor(m[:, :3, :], m[:, :3, :], a3_cols[:, :3, :], MULT)
             staged["m", j] = m
 
         def first_product(j):
@@ -208,7 +208,7 @@ def tile_moe_bdx_glu_sigmoid_kernel(
                     stop=True,
                 )
                 if e in (1, 3):
-                    dht_sb = work.tile([P, PACK, P], F32, name="dht_sb", tag=("m0", "sig5")[e // 2], bufs=1, align_bytes=64)
+                    dht_sb = work.tile([P, PACK, P], F32, name="dht_sb", tag=("m0", "sig6")[e // 2], bufs=1, align_bytes=64)
                 else:
                     dht_sb = work.tile([P, PACK, P], F32, name="dht_sb", bufs=4)
                 nc.scalar.copy(out=dht_sb[:], in_=dht[:].rearrange("s (p t) -> s t p", t=PACK))
@@ -297,7 +297,6 @@ def tile_moe_bdx_glu_sigmoid_kernel(
         slope(0)
         for j in range(NG):
             if j + 1 < NG:
-                shift(j + 1)
                 slope(j + 1)
             if j >= 2:
                 quantise_da(j - 2, 0, GE)

from contextlib import ExitStack

import concourse.mybir as mybir
from concourse.masks import make_identity

K, T, E, C, H, N = 128, 512, 16, 128, 512, 512
S = E * C
FLOPS = 2 * S * (N * H + 2 * H * K)
BYTES = 4 * (N * T + 2 * H * S + S + K * T) + E * (N * H + 2 * H * K) * 17 // 32 + 2 * 128 * (S + 4 * T) // 16

F32 = mybir.dt.float32
BF16 = mybir.dt.bfloat16
I32 = mybir.dt.int32
U32 = mybir.dt.uint32
U16 = mybir.dt.uint16
U8 = mybir.dt.uint8
FP8X4 = mybir.dt.float8_e4m3fn_x4
FP4X4 = mybir.dt.float4_e2m1fn_x4
MULT = mybir.AluOpType.mult
ADD = mybir.AluOpType.add
SUB = mybir.AluOpType.subtract
ACT = mybir.ActivationFunctionType

P = 128
PACK = 4
GE = 2
GS = GE * C
NG = E // GE
LE = 4
LS = LE * C
NL = E // LE


def tile_moe_bdx_glu_sigmoid_kernel(
    tc, dyT, a1, a3, w2_words, w2_scales, w1_words, w1_scales, w3_words, w3_scales, gate, offs, pos1, pos2, pos3, pos4, out
):
    nc = tc.nc
    with ExitStack() as ctx:
        keep = ctx.enter_context(tc.tile_pool(name="keep", bufs=1))
        work = ctx.enter_context(tc.tile_pool(name="work", bufs=2))
        psum = ctx.enter_context(tc.psum_pool(name="psum", bufs=2))

        offs_sb = keep.tile([P, S // 16], U16, name="offs_sb")
        pos_sb = [keep.tile([P, T // 16], U16, name=f"pos_sb{r}") for r in range(4)]
        dy_sb = [keep.tile([P, T], F32, name=f"dy_sb{t}") for t in range(PACK)]
        gate_cuts = [0, LS, 2 * LS, 3 * LS, S]
        gate_sb = [keep.tile([P, gate_cuts[c + 1] - gate_cuts[c]], F32, name=f"gate_sb{c}") for c in range(4)]
        a1_cuts = [0, GS, LS, 2 * LS, 3 * LS, S]
        a1_sb = [keep.tile([P, PACK, a1_cuts[c + 1] - a1_cuts[c]], F32, name=f"a1_sb{c}") for c in range(5)]
        a3_sb = [keep.tile([P, PACK, LS], F32, name=f"a3_sb{c}") for c in range(NL)]
        w2_sb = [keep.tile([P, LE, 2 * H], U8, name=f"w2_sb{c}", align_bytes=64) for c in range(NL)]
        w1_sb = [keep.tile([P, E // 2, 2 * K], U8, name=f"w1_sb{c}", align_bytes=64) for c in range(2)]
        w3_sb = [keep.tile([P, E // 2, 2 * K], U8, name=f"w3_sb{c}", align_bytes=64) for c in range(2)]
        w2_sc_first = keep.tile([P, LE, H], U8, name="w2_sc_first", align_bytes=64)
        w2_sc_rest = keep.tile([P, E - LE, H], U8, name="w2_sc_rest", align_bytes=64)
        w1_sc = keep.tile([P, E, K], U8, name="w1_sc", align_bytes=64)
        w3_sc = keep.tile([P, E, K], U8, name="w3_sc", align_bytes=64)
        ident = keep.tile([P, P], F32, name="ident")
        minus_half = keep.tile([P, 1], F32, name="minus_half")
        dx_sb = keep.tile([P, S], F32, name="dx_sb")
        g_codes = [keep.tile([P, GS], U32, name=f"g_codes{j}", align_bytes=64) for j in range(NG)]
        g_scales = [keep.tile([P, GS], U8, name=f"g_scales{j}", align_bytes=64) for j in range(NG)]

        for plane in (w2_sc_first, w2_sc_rest, w1_sc, w3_sc):
            nc.vector.memset(plane[:].bitcast(I32), 0)
        nc.vector.memset(minus_half[:], -0.5)
        make_identity(nc, ident[:])

        dy_v = dyT.rearrange("(p t) w -> p t w", t=PACK)
        a1_v = a1.rearrange("(p t) w -> p t w", t=PACK)
        a3_v = a3.rearrange("(p t) w -> p t w", t=PACK)

        def load_words(dst, words, e0, e1):
            nc.sync.dma_start(out=dst[:].bitcast(I32), in_=words[e0:e1, 0].rearrange("e p b -> p e b").bitcast(I32))

        def load_scales(plane, scales):
            rows = scales[:, 0].rearrange("e (q r) i -> r q e i", r=4)
            for r in range(4):
                nc.sync.dma_start(out=plane[r:P:32, :, :].bitcast(I32), in_=rows[r].bitcast(I32))

        def load_gate(c):
            nc.sync.dma_start(out=gate_sb[c][:], in_=gate[0:P, gate_cuts[c] : gate_cuts[c + 1]])

        def load_a1(c):
            nc.sync.dma_start(out=a1_sb[c][:], in_=a1_v[:, :, a1_cuts[c] : a1_cuts[c + 1]])

        def load_a3(c):
            nc.sync.dma_start(out=a3_sb[c][:], in_=a3_v[:, :, c * LS : (c + 1) * LS])

        def load_w2(c):
            load_words(w2_sb[c], w2_words, c * LE, (c + 1) * LE)

        nc.sync.dma_start(offs_sb[:], offs)
        nc.sync.dma_start(out=dy_sb[0][:], in_=dy_v[:, 0, :])
        load_gate(0)
        nc.sync.dma_start(out=dy_sb[1][:], in_=dy_v[:, 1, :])
        load_a1(0)
        for t in range(2, PACK):
            nc.sync.dma_start(out=dy_sb[t][:], in_=dy_v[:, t, :])
        load_a1(1)
        load_gate(1)
        load_scales(w2_sc_first, w2_scales[0:LE])
        load_w2(0)
        load_gate(2)
        load_gate(3)
        load_a1(2)
        load_a3(0)
        load_scales(w2_sc_rest, w2_scales[LE:E])
        load_w2(1)
        load_a1(3)
        load_a3(1)
        load_w2(2)
        load_a1(4)
        load_scales(w1_sc, w1_scales)
        load_scales(w3_sc, w3_scales)
        load_words(w1_sb[0], w1_words, 0, E // 2)
        load_words(w3_sb[0], w3_words, 0, E // 2)
        load_w2(3)
        load_a3(2)
        load_a3(3)
        load_words(w1_sb[1], w1_words, E // 2, E)
        load_words(w3_sb[1], w3_words, E // 2, E)
        for r, pos in enumerate((pos1, pos2, pos3, pos4)):
            nc.sync.dma_start(pos_sb[r][:], pos)

        def group_cols(j):
            c, h = divmod(j, LE // GE)
            return c, slice(h * GS, (h + 1) * GS)

        staged = {}

        def gather_plane(j, t):
            c, cols = group_cols(j)
            if t == 0:
                staged["g32", j] = work.tile([P, PACK, GS], F32, name="g32", tag="g32", bufs=4)
            window = dy_sb[t][:].indirect(offs_sb[:, j * GS // 16 : (j + 1) * GS // 16])
            nc.vector.tensor_tensor(staged["g32", j][:, t, :], window, gate_sb[c][:, cols], MULT)

        def gather(j):
            for t in range(PACK - 1 if j < 2 else 0, PACK):
                gather_plane(j, t)
            g32 = staged["g32", j]
            if j >= NG - 2:
                g16 = work.tile([P, GS, PACK], BF16, name="g16", tag=("m0", "sig6")[j - NG + 2], bufs=1, align_bytes=64)
            else:
                g16 = work.tile([P, GS, PACK], BF16, name="g16", bufs=3, align_bytes=64)
            nc.scalar.copy(
                out=g16[:].rearrange("p (c i) t -> p c t i", i=2),
                in_=g32[:].rearrange("p t (c i) -> p c t i", i=2),
            )
            staged["g16", j] = g16

        def quantise_g(j):
            nc.vector.quantize_mx(
                out=g_codes[j][:].bitcast(FP8X4),
                scales=g_scales[j][:],
                in_=staged["g16", j][:].rearrange("p s t -> p (s t)"),
            )

        def sigmoid(j):
            c = max(n for n in range(5) if a1_cuts[n] <= j * GS)
            cols = slice(j * GS - a1_cuts[c], (j + 1) * GS - a1_cuts[c])
            sig = work.tile([P, GS, PACK], F32, name="sig", tag=f"sig{j % 7}", bufs=1, align_bytes=64)
            nc.scalar.activation(
                out=sig[:].rearrange("p (c i) t -> p c t i", i=2),
                in_=a1_sb[c][:, :, cols].rearrange("p t (c i) -> p c t i", i=2),
                func=ACT.Sigmoid,
            )
            staged["sig", j] = sig

        def square(j):
            sig = staged["sig", j]
            sq = work.tile([P, PACK, GS], F32, name="sq", tag=f"pair{j % 5}", bufs=1, align_bytes=64)
            nc.scalar.activation(
                out=sq[:].rearrange("p t (c i) -> p c t i", i=2),
                in_=sig[:].rearrange("p (c i) t -> p c t i", i=2),
                func=ACT.Square,
                bias=minus_half[:],
            )
            staged["sq", j] = sq

        def slope(j):
            c, cols = group_cols(j)
            sq = staged["sq", j]
            a3_cols = a3_sb[c][:, :, cols]
            if j == 0:
                m = work.tile([P, PACK, GS], F32, name="m", tag="m0", bufs=1, align_bytes=64)
                nc.vector.scalar_tensor_tensor(m[:], sq[:], 0.25, a3_cols, SUB, MULT)
            else:
                m = work.tile([P, PACK, GS], F32, name="m", tag=f"sig{(j - 2) % 7}", bufs=1, align_bytes=64)
                nc.vector.scalar_tensor_tensor(m[:, 3:, :], sq[:, 3:, :], 0.25, a3_cols[:, 3:, :], SUB, MULT)
                nc.vector.tensor_scalar_add(m[:, :3, :], sq[:, :3, :], -0.25)
                nc.gpsimd.tensor_tensor(m[:, :3, :], m[:, :3, :], a3_cols[:, :3, :], MULT)
            staged["m", j] = m

        def first_product(j):
            for x in range(GE):
                e = j * GE + x
                slots = slice(x * C, (x + 1) * C)
                dht = psum.tile([P, H], F32, name="dht", bufs=2)
                nc.tensor.matmul_mx(
                    out=dht[:],
                    lhsT=g_codes[j][:, slots].bitcast(FP8X4),
                    lhsT_scale=g_scales[j][:, slots],
                    rhs=w2_sb[e // LE][:, e % LE, :].bitcast(FP4X4),
                    rhs_scale=w2_sc_first[:, e, :] if e < LE else w2_sc_rest[:, e - LE, :],
                    start=True,
                    stop=True,
                )
                if e in (1, 3):
                    dht_sb = work.tile([P, PACK, P], F32, name="dht_sb", tag=("m0", "sig6")[e // 2], bufs=1, align_bytes=64)
                else:
                    dht_sb = work.tile([P, PACK, P], F32, name="dht_sb", bufs=4)
                nc.scalar.copy(out=dht_sb[:], in_=dht[:].rearrange("s (p t) -> s t p", t=PACK))
                staged["dht", e] = dht_sb

        def turn(j):
            for x in range(GE):
                e = j * GE + x
                dh = psum.tile([P, PACK, C], F32, name="dh", bufs=4)
                for t in range(PACK):
                    nc.tensor.transpose(dh[:, t, :], staged["dht", e][:, t, :], ident[:])
                staged["dh", e] = dh

        def gradients(j):
            da = work.tile([P, GE, 2, C, PACK], BF16, name="da", tag=f"pair{(j + 1) % 5}", bufs=1, align_bytes=64)
            for x in range(GE):
                slots = slice(x * C, (x + 1) * C)
                dh = staged["dh", j * GE + x]
                nc.vector.scalar_tensor_tensor(
                    da[:, x, 1], staged["sig", j][:, slots, :], -1.0, dh[:].rearrange("p t s -> p s t"), MULT, MULT
                )
            for x in range(GE):
                slots = slice(x * C, (x + 1) * C)
                dh = staged["dh", j * GE + x]
                nc.vector.tensor_tensor(
                    da[:, x, 0].rearrange("p (c i) t -> p c t i", i=2),
                    dh[:].rearrange("p t (c i) -> p c t i", i=2),
                    staged["m", j][:, :, slots].rearrange("p t (c i) -> p c t i", i=2),
                    MULT,
                )
            staged["da", j] = da

        def quantise_da(j, x0, x1):
            width = x1 - x0
            da_codes = work.tile([P, width, 2, C], U32, name="da_codes", bufs=3, align_bytes=64)
            da_scales = work.tile([P, width, 2, C], U8, name="da_scales", bufs=3, align_bytes=64)
            nc.vector.quantize_mx(
                out=da_codes[:].rearrange("p x m s -> p (x m s)").bitcast(FP8X4),
                scales=da_scales[:].rearrange("p x m s -> p (x m s)"),
                in_=staged["da", j][:, x0:x1].rearrange("p x m s t -> p (x m s t)"),
            )
            staged["codes", j, x0] = (da_codes, da_scales)

        def second_product(j, x0, x1):
            width = x1 - x0
            da_codes, da_scales = staged["codes", j, x0]
            dx = psum.tile([P, width * C], F32, name="dx", bufs=2)
            for x in range(width):
                e = j * GE + x0 + x
                for which, (words, plane) in enumerate(((w1_sb, w1_sc), (w3_sb, w3_sc))):
                    nc.tensor.matmul_mx(
                        out=dx[:, x * C : (x + 1) * C],
                        lhsT=words[e // (E // 2)][:, e % (E // 2), :].bitcast(FP4X4),
                        lhsT_scale=plane[:, e, :],
                        rhs=da_codes[:, x, which, :].bitcast(FP8X4),
                        rhs_scale=da_scales[:, x, which, :],
                        start=(which == 0),
                        stop=(which == 1),
                    )
            first = (j * GE + x0) * C
            nc.scalar.activation(out=dx_sb[:, first : first + width * C], in_=dx[:], func=ACT.Copy, scale=-1.0)

        early = [
            [(sigmoid, 1)],
            [(square, 1)],
            [(first_product, 0), (turn, 0)],
            [(sigmoid, 2), (square, 2)],
            [(first_product, 1), (turn, 1)],
            [(sigmoid, 3)],
            [(square, 3)],
        ]
        for t in range(PACK - 1):
            gather_plane(0, t)
            gather_plane(1, t)
        sigmoid(0)
        square(0)
        for j in range(NG + 1):
            if j < NG:
                gather(j)
            if j >= 1:
                quantise_g(j - 1)
            if 1 <= j < NG:
                for step, group in early[j - 1]:
                    step(group)

        slope(0)
        for j in range(NG):
            if j + 1 < NG:
                slope(j + 1)
            if j >= 2:
                quantise_da(j - 2, 0, GE)
            if j == NG - 1:
                quantise_da(j - 1, 0, GE)
            if j + 2 < NG:
                first_product(j + 2)
            if j + 4 < NG:
                sigmoid(j + 4)
                square(j + 4)
            if 1 < j + 1 < NG:
                turn(j + 1)
            if j >= 2:
                second_product(j - 2, 0, GE)
            if j == NG - 1:
                second_product(j - 1, 0, GE)
            gradients(j)
        for x in range(GE):
            quantise_da(NG - 1, x, x + 1)
            second_product(NG - 1, x, x + 1)

        half = T // 2
        sums = [None, None]
        for r in range(4):
            for h in range(2):
                window = dx_sb[:].indirect(pos_sb[r][:, h * half // 16 : (h + 1) * half // 16])
                acc = work.tile([P, half], F32, name="acc", tag="g32", bufs=4)
                if r == 0:
                    nc.vector.tensor_copy(acc[:], window)
                else:
                    nc.vector.tensor_tensor(acc[:], window, sums[h][:], ADD)
                sums[h] = acc
                if r == 3:
                    nc.sync.dma_start(out=out[:, h * half : (h + 1) * half], in_=acc[:])
